import numpy as np
CORES = [129,145,193,257,273,321,385,401,449]
N = 9
W = 64
def setup_inputs(rng):
    amp = 0.5 + 1.5 * rng.random((2, N, 128, 1), dtype=np.float32)
    return {"u": amp[0] * rng.standard_normal((N, 128, W), dtype=np.float32), "b": amp[1] * rng.standard_normal((N, 128, W), dtype=np.float32)}
def setup_inputs_big(rng):
    d = setup_inputs(rng)
    for k in ("u", "b"): d[k] = (d[k].astype(np.float32) * 1024.0).astype(d[k].dtype)
    return d
def setup_inputs_small(rng):
    d = setup_inputs(rng)
    for k in ("u", "b"): d[k] = (d[k].astype(np.float32) * (1 / 1024.0)).astype(d[k].dtype)
    return d
def setup_inputs_apart(rng):
    d = setup_inputs(rng)
    f = (10.0 ** rng.permutation(np.linspace(-1.5, 1.5, N))).astype(np.float32).reshape(N, 1, 1)
    for k in ("u", "b"): d[k] = (d[k].astype(np.float32) * f).astype(d[k].dtype)
    return d
def reference(u, b):
    g = np.concatenate(list(u.astype(np.float64)), axis=1); bb = np.concatenate(list(b.astype(np.float64)), axis=1)
    p = np.concatenate([g[:, -2:], g, g[:, :2]], axis=1)
    n = 0.125 * (p[:, :-4] + p[:, 1:-3] + p[:, 3:-1] + p[:, 4:]) + 0.5 * bb
    d = n - g
    s = np.stack([(d ** 2).mean(axis=1), np.abs(d).max(axis=1)], axis=1)
    return {"y": np.stack([n[:, W * r:W * r + W] for r in range(N)]).astype(np.float32), "s": np.broadcast_to(s.astype(np.float32), (N, 128, 2))}

@@ -1,0 +1,251 @@
+from concourse.bass import DstId, RemoteDMATransfer
+from concourse.mybir import AluOpType
+
+N, W = 9, 64
+K = 16
+SCRATCH = {
+    "F": ("sbuf", [128, W + 8], "float32"),
+    "Bz": ("sbuf", [128, W + 8], "float32"),
+    "A": ("sbuf", [128, W + 8], "float32"),
+    "E": ("sbuf", [128, W + 4], "float32"),
+    "C8": ("sbuf", [128, W + 4], "float32"),
+    "D": ("sbuf", [128, W - 4], "float32"),
+    "SQ": ("sbuf", [128, W - 4], "float32"),
+    "AB": ("sbuf", [128, W - 4], "float32"),
+    "Y": ("sbuf", [128, W], "float32"),
+    "YW": ("sbuf", [128, 4], "float32"),
+    "L": ("sbuf", [128, N, K], "float32"),
+    "HQ": ("sbuf", [128, 4], "float32"),
+    "RL": ("sbuf", [128, 4], "float32"),
+    "ZH": ("sbuf", [128, N, 4], "float32"),
+    "DB": ("sbuf", [128, N, 4], "float32"),
+    "NDB": ("sbuf", [128, N, 4], "float32"),
+    "SQB": ("sbuf", [128, N, 4], "float32"),
+    "ABB": ("sbuf", [128, N, 4], "float32"),
+    "S1": ("sbuf", [128, N, 4], "float32"),
+    "M1": ("sbuf", [128, N, 4], "float32"),
+    "XX": ("sbuf", [128, 4], "float32"),
+    "RES": ("sbuf", [128, 4], "float32"),
+    "CS": ("sbuf", [128, 4], "float32"),
+    "PT": ("psum", [128, W + 4], "float32"),
+    "PT8": ("psum", [128, W + 4], "float32"),
+    "PHB": ("psum", [128, W + 4], "float32"),
+    "PC2": ("psum", [128, W + 4], "float32"),
+    "PZ": ("psum", [128, W - 4], "float32"),
+    "PND": ("psum", [128, W - 4], "float32"),
+    "PY": ("psum", [128, W], "float32"),
+}
+SEMAPHORES = ["lu", "lb", "ms", "v", "msg", "arr", "hq", "fin", "res", "yv", "yw", "sent", "sts", "sty"]
+
+
+def _bits(m):
+    return [1 << i for i in range(16) if (m >> i) & 1]
+
+
+def _parts(m, n):
+    b = _bits(m)
+    size = 1
+    while size * 2 * n <= len(b):
+        size *= 2
+    return [sum(b[i * size:(i + 1) * size]) for i in range(n)], size
+
+
+def rank_program(g, core, T, topo):
+    rank = T.rank_of(core)
+    if rank is None:
+        return
+    cores = list(T.cores)
+    sem = T.sem
+    add, sub, mul, mx = AluOpType.add, AluOpType.subtract, AluOpType.mult, AluOpType.max
+    others = lambda r: [x for x in range(N) if x != r]
+    ok = lambda a, b: topo.may_write(cores[a], cores[b])
+
+    hubs = [r for r in range(N) if all(ok(r, x) and ok(x, r) for x in others(r))]
+    clients = [r for r in range(N) if r not in hubs]
+    load = dict((h, 0) for h in hubs)
+    hub_of = {}
+    for c in clients:
+        h = min(hubs, key=lambda h: (load[h], 0 if topo.chip(cores[h]) == topo.chip(cores[c]) else 1, h))
+        hub_of[c] = h
+        load[h] += 1
+    left = lambda r: (r - 1) % N
+    right = lambda r: (r + 1) % N
+
+    def common_mask(src, dsts):
+        m = topo.mask(cores[src], cores[dsts[0]])
+        for d in dsts[1:]:
+            m &= topo.mask(cores[src], cores[d])
+        return m
+
+    def halo_plan(x):
+        t = []
+        if right(x) in clients and ok(x, right(x)):
+            t.append((right(x), 14, 0))
+        if left(x) in clients and ok(x, left(x)):
+            t.append((left(x), 8, 2))
+        if not t:
+            return []
+        masks, size = _parts(common_mask(x, [d for d, _, _ in t]), len(t))
+        return [(d, s, o, masks[i], size) for i, (d, s, o) in enumerate(t)]
+
+    def hub_plan(h):
+        plan = (None, 0, 2, 0, None, None, None)
+        for c in clients:
+            if hub_of[c] != h:
+                continue
+            if not ok(left(c), c):
+                plan = (left(c), 12, 4, 0, 2, c, "L")
+            elif not ok(right(c), c):
+                plan = (right(c), 8, 4, 2, 0, c, "R")
+        return plan
+
+    def dst(d):
+        rid, pid = topo.addr(cores[d], core)
+        return DstId(rid=rid, pnc=pid)
+
+    is_hub = rank in hubs
+    F, Bz, A, E, C8, D, SQ, AB, Y, L = T.F, T.Bz, T.A, T.E, T.C8, T.D, T.SQ, T.AB, T.Y, T.L
+    vec = g.vector
+
+    g.sync.dma_start(F[:, 4:4 + W], T.u[:, :]).then_inc(sem.lu, 16)
+    g.scalar.dma_start(Bz[:, 4:4 + W], T.b[:, :]).then_inc(sem.lb, 16)
+
+    fills = [(F[:, 0:4], 0.0), (F[:, W + 4:W + 8], 0.0), (Bz[:, 0:4], 0.0), (Bz[:, W + 4:W + 8], 0.0),
+             (C8[:, :], 0.125), (T.PC2[:, :], 0.5), (T.PZ[:, :], 0.0)]
+    if is_hub:
+        fills += [(T.ZH[:, :, :], 0.0), (T.CS[:, 0:1], -1.0 / (N * W)), (T.CS[:, 1:2], 1.0)]
+    for ap, c in fills:
+        vec.memset(ap, c).then_inc(sem.ms, 1)
+    vec.wait_ge(sem.ms, len(fills))
+
+    st = {"v": 0, "w": 0}
+
+    def vwait():
+        if st["w"] < st["v"]:
+            vec.wait_ge(sem.v, st["v"])
+            st["w"] = st["v"]
+
+    def tt(out, a, b, op, dep=True, sig=None):
+        if dep:
+            vwait()
+        ins = vec.tensor_tensor(out, a, b, op)
+        if sig is None:
+            ins.then_inc(sem.v, 1)
+            st["v"] += 1
+        else:
+            ins.then_inc(sig, 1)
+
+    X = W + 4
+    vec.wait_ge(sem.lu, 16)
+    tt(A[:, 0:X + 3], F[:, 0:X + 3], F[:, 1:X + 4], add, dep=False)
+    vec.wait_ge(sem.lb, 16)
+    tt(T.PHB[:, :], Bz[:, 2:2 + X], T.PC2[:, :], mul, dep=False)
+    tt(T.PT[:, :], A[:, 0:X], A[:, 3:X + 3], add)
+    tt(E[:, :], T.PHB[:, :], F[:, 2:2 + X], sub, dep=False)
+    tt(T.PT8[:, :], T.PT[:, :], C8[:, :], mul)
+    tt(D[:, :], T.PT8[:, 4:W], E[:, 4:W], add)
+    tt(L[:, rank, 8:12], T.PT8[:, 0:4], E[:, 0:4], add, dep=False, sig=sem.msg)
+    tt(L[:, rank, 12:16], T.PT8[:, W:W + 4], E[:, W:W + 4], add, dep=False, sig=sem.msg)
+    tt(T.PND[:, :], T.PZ[:, :], D[:, :], sub)
+    tt(SQ[:, :], D[:, :], T.PND[:, :], mul)
+    tt(AB[:, :], D[:, :], T.PND[:, :], mx, dep=False)
+    n = W - 4
+    while n > 8:
+        h = n // 2
+        tt(SQ[:, 0:h], SQ[:, 0:h], SQ[:, n - h:n], add)
+        tt(AB[:, 0:h], AB[:, 0:h], AB[:, n - h:n], mx, dep=False)
+        n -= h
+    tt(L[:, rank, 0:4], SQ[:, 0:4], SQ[:, 4:8], add, sig=sem.msg)
+    tt(L[:, rank, 4:8], AB[:, 0:4], AB[:, 4:8], mx, dep=False, sig=sem.msg)
+
+    sent = 0
+    to = [h for h in hubs if h != rank]
+    m1, e1 = _parts(common_mask(rank, to), 1)
+    g.wait_ge(sem.msg, 4)
+    g.remote_dma_fused([RemoteDMATransfer(dst_ids=[dst(h) for h in to], dma_engine_mask=m1[0], remote_sem=sem.arr,
+                                          srcs=[L[:, rank, :]], dsts=[L[:, rank, :] for h in to])], local_sem=sem.sent)
+    sent += e1
+    hp = halo_plan(rank)
+    if hp:
+        g.remote_dma_fused([RemoteDMATransfer(dst_ids=[dst(d)], dma_engine_mask=m, remote_sem=sem.hq,
+                                              srcs=[L[:, rank, s:s + 2]], dsts=[T.HQ[:, o:o + 2]])
+                            for d, s, o, m, _ in hp], local_sem=sem.sent)
+        sent += sum(e for _, _, _, _, e in hp)
+
+    tt(T.PY[:, :], T.PT8[:, 2:2 + W], E[:, 2:2 + W], add, dep=False)
+    tt(Y[:, :], T.PY[:, :], F[:, 4:4 + W], add)
+
+    if is_hub:
+        slot, c0, width, s_off, q_off, _, _ = hub_plan(rank)
+        res = T.RES[:, 0:2] if slot is None else L[:, slot, c0 + s_off:c0 + s_off + 2]
+        src = T.RES[:, 0:2] if slot is None else L[:, slot, c0:c0 + width]
+        vec.wait_ge(sem.arr, sum(_parts(common_mask(x, [h for h in hubs if h != x]), 1)[1] for x in others(rank)))
+        vec.wait_ge(sem.msg, 4)
+        DB, NDB, SQB, ABB, S1, M1, XX = T.DB, T.NDB, T.SQB, T.ABB, T.S1, T.M1, T.XX
+        tt(DB[:, 0:N - 1, :], L[:, 0:N - 1, 12:16], L[:, 1:N, 8:12], add)
+        tt(DB[:, N - 1, :], L[:, N - 1, 12:16], L[:, 0, 8:12], add, dep=False)
+        tt(NDB[:, :, :], T.ZH[:, :, :], DB[:, :, :], sub)
+        tt(SQB[:, :, :], DB[:, :, :], NDB[:, :, :], mul)
+        tt(ABB[:, :, :], DB[:, :, :], NDB[:, :, :], mx, dep=False)
+        tt(S1[:, :, :], L[:, :, 0:4], SQB[:, :, :], add)
+        tt(M1[:, :, :], L[:, :, 4:8], ABB[:, :, :], mx, dep=False)
+        n = N
+        while n > 2:
+            h = n // 2
+            tt(S1[:, 0:h, :], S1[:, 0:h, :], S1[:, n - h:n, :], add)
+            tt(M1[:, 0:h, :], M1[:, 0:h, :], M1[:, n - h:n, :], mx, dep=False)
+            n -= h
+        tt(S1[:, 0, :], S1[:, 0, :], S1[:, 1, :], add)
+        tt(M1[:, 0, :], M1[:, 0, :], M1[:, 1, :], mx, dep=False)
+        tt(S1[:, 0, 0:2], S1[:, 0, 0:2], S1[:, 0, 2:4], add)
+        tt(M1[:, 0, 0:2], M1[:, 0, 0:2], M1[:, 0, 2:4], mx, dep=False)
+        tt(XX[:, 0:1], S1[:, 0, 0:1], S1[:, 0, 1:2], add)
+        tt(XX[:, 1:2], M1[:, 0, 0:1], M1[:, 0, 1:2], mx, dep=False)
+        tt(res, XX[:, 0:2], T.CS[:, 0:2], mul, sig=sem.res)
+        mine = [c for c in clients if hub_of[c] == rank]
+        m2, e2 = _parts(common_mask(rank, mine), 1)
+        g.wait_ge(sem.res, 1)
+        g.remote_dma_fused([RemoteDMATransfer(dst_ids=[dst(c) for c in mine], dma_engine_mask=m2[0], remote_sem=sem.fin,
+                                              srcs=[src], dsts=[T.RL[:, 0:width] for c in mine])], local_sem=sem.sent)
+        sent += e2
+        g.sync.wait_ge(sem.res, 1)
+        g.sync.dma_start(T.s[:, :], res).then_inc(sem.sts, 16)
+        tt(Y[:, 0:2], Y[:, 0:2], L[:, left(rank), 14:16], add, sig=sem.yv)
+        tt(Y[:, W - 2:W], Y[:, W - 2:W], L[:, right(rank), 8:10], add, dep=False, sig=sem.yv)
+        g.scalar.wait_ge(sem.yv, 2)
+        g.scalar.dma_start(T.y[:, :], Y[:, :]).then_inc(sem.sty, 16)
+        stores = 1
+    else:
+        hub = hub_of[rank]
+        slot, c0, width, s_off, q_off, seam, side = hub_plan(hub)
+        fin = _parts(common_mask(hub, [c for c in clients if hub_of[c] == hub]), 1)[1]
+        got = {}
+        for x in (left(rank), right(rank)):
+            for d, s, o, m, e in halo_plan(x):
+                if d == rank:
+                    got[o] = e
+        vec.wait_ge(sem.hq, sum(got.values()))
+        first = True
+        if 0 in got:
+            tt(Y[:, 0:2], Y[:, 0:2], T.HQ[:, 0:2], add, dep=first, sig=sem.yv)
+            first = False
+        if 2 in got:
+            tt(Y[:, W - 2:W], Y[:, W - 2:W], T.HQ[:, 2:4], add, dep=first, sig=sem.yv)
+        lo, hi = (0 if 0 in got else 2), (W if 2 in got else W - 2)
+        g.scalar.wait_ge(sem.yv, len(got))
+        g.scalar.dma_start(T.y[:, lo:hi], Y[:, lo:hi]).then_inc(sem.sty, 16)
+        stores = 1
+        g.sync.wait_ge(sem.fin, fin)
+        g.sync.dma_start(T.s[:, :], T.RL[:, s_off:s_off + 2]).then_inc(sem.sts, 16)
+        if seam == rank:
+            a = 0 if side == "L" else W - 2
+            vec.wait_ge(sem.fin, fin)
+            tt(T.YW[:, 0:2], Y[:, a:a + 2], T.RL[:, q_off:q_off + 2], add, dep=False, sig=sem.yw)
+            g.scalar.wait_ge(sem.yw, 1)
+            g.scalar.dma_start(T.y[:, a:a + 2], T.YW[:, 0:2]).then_inc(sem.sty, 16)
+            stores = 2
+
+    vwait()
+    g.wait_ge(sem.sent, sent)
+    g.sync.wait_ge(sem.sts, 16)
+    g.scalar.wait_ge(sem.sty, 16 * stores)

@@ -13,10 +13,11 @@ SCRATCH = {
     "SQ": ("sbuf", [128, W - 4], "float32"),
     "AB": ("sbuf", [128, W - 4], "float32"),
     "Y": ("sbuf", [128, W], "float32"),
-    "YW": ("sbuf", [128, 4], "float32"),
     "L": ("sbuf", [128, N, K], "float32"),
+    "HR": ("sbuf", [128, 4], "float32"),
+    "G": ("sbuf", [128, 4], "float32"),
     "HQ": ("sbuf", [128, 4], "float32"),
-    "RL": ("sbuf", [128, 4], "float32"),
+    "SD": ("dram", [128, 2], "float32"),
     "ZH": ("sbuf", [128, N, 4], "float32"),
     "DB": ("sbuf", [128, N, 4], "float32"),
     "NDB": ("sbuf", [128, N, 4], "float32"),
@@ -35,7 +36,7 @@ SCRATCH = {
     "PND": ("psum", [128, W - 4], "float32"),
     "PY": ("psum", [128, W], "float32"),
 }
-SEMAPHORES = ["lu", "lb", "ms", "v", "msg", "arr", "hq", "fin", "res", "yv", "yw", "sent", "sts", "sty"]
+SEMAPHORES = ["lu", "lb", "ms", "v", "msg", "arr", "hr", "hq", "fin", "res", "yv", "sent", "sts", "sty"]
 
 
 def _bits(m):
@@ -77,27 +78,28 @@ def rank_program(g, core, T, topo):
             m &= topo.mask(cores[src], cores[d])
         return m
 
-    def halo_plan(x):
-        t = []
-        if right(x) in clients and ok(x, right(x)):
-            t.append((right(x), 14, 0))
-        if left(x) in clients and ok(x, left(x)):
-            t.append((left(x), 8, 2))
+    def spread(x, t):
         if not t:
             return []
-        masks, size = _parts(common_mask(x, [d for d, _, _ in t]), len(t))
-        return [(d, s, o, masks[i], size) for i, (d, s, o) in enumerate(t)]
+        masks, size = _parts(common_mask(x, [e[0] for e in t]), len(t))
+        return [e + (masks[i], size) for i, e in enumerate(t)]
 
-    def hub_plan(h):
-        plan = (None, 0, 2, 0, None, None, None)
+    def halo_plan(x):
+        t = []
+        if ok(x, right(x)):
+            t.append((right(x), 4 + W - 2, 0))
+        if ok(x, left(x)):
+            t.append((left(x), 4, 2))
+        return spread(x, t)
+
+    def pass_plan(h):
+        t = []
         for c in clients:
-            if hub_of[c] != h:
-                continue
-            if not ok(left(c), c):
-                plan = (left(c), 12, 4, 0, 2, c, "L")
-            elif not ok(right(c), c):
-                plan = (right(c), 8, 4, 2, 0, c, "R")
-        return plan
+            if hub_of[c] == h and not ok(left(c), c):
+                t.append((c, left(c), 14, 0))
+            if hub_of[c] == h and not ok(right(c), c):
+                t.append((c, right(c), 8, 2))
+        return spread(h, t)
 
     def dst(d):
         rid, pid = topo.addr(cores[d], core)
@@ -118,7 +120,7 @@ def rank_program(g, core, T, topo):
         vec.memset(ap, c).then_inc(sem.ms, 1)
     vec.wait_ge(sem.ms, len(fills))
 
-    st = {"v": 0, "w": 0}
+    st = {"v": 0, "w": 0, "sent": 0}
 
     def vwait():
         if st["w"] < st["v"]:
@@ -134,6 +136,13 @@ def rank_program(g, core, T, topo):
             st["v"] += 1
         else:
             ins.then_inc(sig, 1)
+
+    hp = halo_plan(rank)
+    g.wait_ge(sem.lu, 16)
+    g.remote_dma_fused([RemoteDMATransfer(dst_ids=[dst(d)], dma_engine_mask=m, remote_sem=sem.hr,
+                                          srcs=[F[:, s:s + 2]], dsts=[T.HR[:, o:o + 2]])
+                        for d, s, o, m, _ in hp], local_sem=sem.sent)
+    st["sent"] += sum(p[4] for p in hp)
 
     X = W + 4
     vec.wait_ge(sem.lu, 16)
@@ -158,28 +167,40 @@ def rank_program(g, core, T, topo):
     tt(L[:, rank, 0:4], SQ[:, 0:4], SQ[:, 4:8], add, sig=sem.msg)
     tt(L[:, rank, 4:8], AB[:, 0:4], AB[:, 4:8], mx, dep=False, sig=sem.msg)
 
-    sent = 0
     to = [h for h in hubs if h != rank]
     m1, e1 = _parts(common_mask(rank, to), 1)
     g.wait_ge(sem.msg, 4)
     g.remote_dma_fused([RemoteDMATransfer(dst_ids=[dst(h) for h in to], dma_engine_mask=m1[0], remote_sem=sem.arr,
                                           srcs=[L[:, rank, :]], dsts=[L[:, rank, :] for h in to])], local_sem=sem.sent)
-    sent += e1
-    hp = halo_plan(rank)
-    if hp:
-        g.remote_dma_fused([RemoteDMATransfer(dst_ids=[dst(d)], dma_engine_mask=m, remote_sem=sem.hq,
-                                              srcs=[L[:, rank, s:s + 2]], dsts=[T.HQ[:, o:o + 2]])
-                            for d, s, o, m, _ in hp], local_sem=sem.sent)
-        sent += sum(e for _, _, _, _, e in hp)
+    st["sent"] += e1
 
     tt(T.PY[:, :], T.PT8[:, 2:2 + W], E[:, 2:2 + W], add, dep=False)
     tt(Y[:, :], T.PY[:, :], F[:, 4:4 + W], add)
+    raw_l, raw_r = ok(left(rank), rank), ok(right(rank), rank)
+    vec.wait_ge(sem.hr, sum(p[4] for x in (left(rank), right(rank)) for p in halo_plan(x) if p[0] == rank))
+    lo, hi = (0 if raw_l else 2), (4 if raw_r else 2)
+    G = T.G
+    tt(G[:, lo:hi], T.HR[:, lo:hi], C8[:, lo:hi], mul, dep=False)
+    if raw_l:
+        tt(Y[:, 0:2], Y[:, 0:2], G[:, 0:2], add)
+    if raw_r:
+        tt(Y[:, W - 2:W], Y[:, W - 2:W], G[:, 2:4], add, dep=not raw_l)
+    if raw_l:
+        tt(Y[:, 0:1], Y[:, 0:1], G[:, 1:2], add, sig=sem.yv)
+    if raw_r:
+        tt(Y[:, W - 1:W], Y[:, W - 1:W], G[:, 2:3], add, dep=not raw_l, sig=sem.yv)
 
     if is_hub:
-        slot, c0, width, s_off, q_off, _, _ = hub_plan(rank)
-        res = T.RES[:, 0:2] if slot is None else L[:, slot, c0 + s_off:c0 + s_off + 2]
-        src = T.RES[:, 0:2] if slot is None else L[:, slot, c0:c0 + width]
-        vec.wait_ge(sem.arr, sum(_parts(common_mask(x, [h for h in hubs if h != x]), 1)[1] for x in others(rank)))
+        res = T.RES[:, 0:2]
+        arrived = sum(_parts(common_mask(x, [h for h in hubs if h != x]), 1)[1] for x in others(rank))
+        pp = pass_plan(rank)
+        if pp:
+            g.wait_ge(sem.arr, arrived)
+            g.remote_dma_fused([RemoteDMATransfer(dst_ids=[dst(d)], dma_engine_mask=m, remote_sem=sem.hq,
+                                                  srcs=[L[:, sl, s:s + 2]], dsts=[T.HQ[:, o:o + 2]])
+                                for d, sl, s, o, m, _ in pp], local_sem=sem.sent)
+            st["sent"] += sum(p[5] for p in pp)
+        vec.wait_ge(sem.arr, arrived)
         vec.wait_ge(sem.msg, 4)
         DB, NDB, SQB, ABB, S1, M1, XX = T.DB, T.NDB, T.SQB, T.ABB, T.S1, T.M1, T.XX
         tt(DB[:, 0:N - 1, :], L[:, 0:N - 1, 12:16], L[:, 1:N, 8:12], add)
@@ -206,46 +227,24 @@ def rank_program(g, core, T, topo):
         m2, e2 = _parts(common_mask(rank, mine), 1)
         g.wait_ge(sem.res, 1)
         g.remote_dma_fused([RemoteDMATransfer(dst_ids=[dst(c) for c in mine], dma_engine_mask=m2[0], remote_sem=sem.fin,
-                                              srcs=[src], dsts=[T.RL[:, 0:width] for c in mine])], local_sem=sem.sent)
-        sent += e2
+                                              srcs=[res], dsts=[T.SD[:, :] for c in mine])], local_sem=sem.sent)
+        st["sent"] += e2
         g.sync.wait_ge(sem.res, 1)
         g.sync.dma_start(T.s[:, :], res).then_inc(sem.sts, 16)
-        tt(Y[:, 0:2], Y[:, 0:2], L[:, left(rank), 14:16], add, sig=sem.yv)
-        tt(Y[:, W - 2:W], Y[:, W - 2:W], L[:, right(rank), 8:10], add, dep=False, sig=sem.yv)
-        g.scalar.wait_ge(sem.yv, 2)
-        g.scalar.dma_start(T.y[:, :], Y[:, :]).then_inc(sem.sty, 16)
-        stores = 1
     else:
         hub = hub_of[rank]
-        slot, c0, width, s_off, q_off, seam, side = hub_plan(hub)
         fin = _parts(common_mask(hub, [c for c in clients if hub_of[c] == hub]), 1)[1]
-        got = {}
-        for x in (left(rank), right(rank)):
-            for d, s, o, m, e in halo_plan(x):
-                if d == rank:
-                    got[o] = e
-        vec.wait_ge(sem.hq, sum(got.values()))
-        first = True
-        if 0 in got:
-            tt(Y[:, 0:2], Y[:, 0:2], T.HQ[:, 0:2], add, dep=first, sig=sem.yv)
-            first = False
-        if 2 in got:
-            tt(Y[:, W - 2:W], Y[:, W - 2:W], T.HQ[:, 2:4], add, dep=first, sig=sem.yv)
-        lo, hi = (0 if 0 in got else 2), (W if 2 in got else W - 2)
-        g.scalar.wait_ge(sem.yv, len(got))
-        g.scalar.dma_start(T.y[:, lo:hi], Y[:, lo:hi]).then_inc(sem.sty, 16)
-        stores = 1
+        for p in pass_plan(hub):
+            if p[0] == rank:
+                a = 0 if p[3] == 0 else W - 2
+                vec.wait_ge(sem.hq, p[5])
+                tt(Y[:, a:a + 2], Y[:, a:a + 2], T.HQ[:, p[3]:p[3] + 2], add, sig=sem.yv)
         g.sync.wait_ge(sem.fin, fin)
-        g.sync.dma_start(T.s[:, :], T.RL[:, s_off:s_off + 2]).then_inc(sem.sts, 16)
-        if seam == rank:
-            a = 0 if side == "L" else W - 2
-            vec.wait_ge(sem.fin, fin)
-            tt(T.YW[:, 0:2], Y[:, a:a + 2], T.RL[:, q_off:q_off + 2], add, dep=False, sig=sem.yw)
-            g.scalar.wait_ge(sem.yw, 1)
-            g.scalar.dma_start(T.y[:, a:a + 2], T.YW[:, 0:2]).then_inc(sem.sty, 16)
-            stores = 2
+        g.sync.dma_start(T.s[:, :], T.SD[:, :]).then_inc(sem.sts, 16)
+    g.scalar.wait_ge(sem.yv, 2)
+    g.scalar.dma_start(T.y[:, :], Y[:, :]).then_inc(sem.sty, 16)
 
     vwait()
-    g.wait_ge(sem.sent, sent)
+    g.wait_ge(sem.sent, st["sent"])
     g.sync.wait_ge(sem.sts, 16)
-    g.scalar.wait_ge(sem.sty, 16 * stores)
+    g.scalar.wait_ge(sem.sty, 16)

@@ -1,54 +1,40 @@
 from concourse.bass import DstId, RemoteDMATransfer
-from concourse.mybir import AluOpType
+from concourse.mybir import AluOpType, AxisListType, ActivationFunctionType
 
 N, W = 9, 64
-K = 16
+K = 12
+X = W + 4
 SCRATCH = {
     "F": ("sbuf", [128, W + 8], "float32"),
     "Bz": ("sbuf", [128, W + 8], "float32"),
     "A": ("sbuf", [128, W + 8], "float32"),
-    "E": ("sbuf", [128, W + 4], "float32"),
-    "C8": ("sbuf", [128, W + 4], "float32"),
+    "U8": ("sbuf", [128, X], "float32"),
+    "XS": ("sbuf", [128, X], "float32"),
     "D": ("sbuf", [128, W - 4], "float32"),
     "SQ": ("sbuf", [128, W - 4], "float32"),
-    "AB": ("sbuf", [128, W - 4], "float32"),
+    "HB": ("sbuf", [128, W], "float32"),
     "Y": ("sbuf", [128, W], "float32"),
     "L": ("sbuf", [128, N, K], "float32"),
     "HR": ("sbuf", [128, 4], "float32"),
     "G": ("sbuf", [128, 4], "float32"),
-    "HQ": ("sbuf", [128, 4], "float32"),
+    "RL": ("sbuf", [128, 4], "float32"),
     "SD": ("dram", [128, 2], "float32"),
-    "ZH": ("sbuf", [128, N, 4], "float32"),
-    "DB": ("sbuf", [128, N, 4], "float32"),
-    "NDB": ("sbuf", [128, N, 4], "float32"),
-    "SQB": ("sbuf", [128, N, 4], "float32"),
-    "ABB": ("sbuf", [128, N, 4], "float32"),
-    "S1": ("sbuf", [128, N, 4], "float32"),
-    "M1": ("sbuf", [128, N, 4], "float32"),
-    "XX": ("sbuf", [128, 4], "float32"),
+    "DB": ("sbuf", [128, 4 * N], "float32"),
+    "J1": ("sbuf", [128, N], "float32"),
+    "J2": ("sbuf", [128, 4 * N], "float32"),
+    "SS": ("sbuf", [128, 4], "float32"),
+    "MM": ("sbuf", [128, 4], "float32"),
     "RES": ("sbuf", [128, 4], "float32"),
-    "CS": ("sbuf", [128, 4], "float32"),
-    "PT": ("psum", [128, W + 4], "float32"),
-    "PT8": ("psum", [128, W + 4], "float32"),
-    "PHB": ("psum", [128, W + 4], "float32"),
-    "PC2": ("psum", [128, W + 4], "float32"),
-    "PZ": ("psum", [128, W - 4], "float32"),
-    "PND": ("psum", [128, W - 4], "float32"),
-    "PY": ("psum", [128, W], "float32"),
+    "PB": ("psum", [128, 512], "float32"),
+    "PT": ("psum", [128, 512], "float32"),
+    "PY": ("psum", [128, 512], "float32"),
 }
-SEMAPHORES = ["lu", "lb", "ms", "v", "msg", "arr", "hr", "hq", "fin", "res", "yv", "sent", "sts", "sty"]
+SEMAPHORES = ["lu", "lb", "ms", "v", "sa", "hb", "d", "msg", "arr", "hr", "rl", "db", "sf", "fin", "res", "yv", "sent",
+              "sts", "sty"]
 
 
-def _bits(m):
-    return [1 << i for i in range(16) if (m >> i) & 1]
-
-
-def _parts(m, n):
-    b = _bits(m)
-    size = 1
-    while size * 2 * n <= len(b):
-        size *= 2
-    return [sum(b[i * size:(i + 1) * size]) for i in range(n)], size
+def _count(m):
+    return sum((m >> i) & 1 for i in range(16))
 
 
 def rank_program(g, core, T, topo):
@@ -57,7 +43,9 @@ def rank_program(g, core, T, topo):
         return
     cores = list(T.cores)
     sem = T.sem
-    add, sub, mul, mx = AluOpType.add, AluOpType.subtract, AluOpType.mult, AluOpType.max
+    add, mul, mx = AluOpType.add, AluOpType.mult, AluOpType.max
+    AX = AxisListType.X
+    ACT = ActivationFunctionType
     others = lambda r: [x for x in range(N) if x != r]
     ok = lambda a, b: topo.may_write(cores[a], cores[b])
 
@@ -78,173 +66,138 @@ def rank_program(g, core, T, topo):
             m &= topo.mask(cores[src], cores[d])
         return m
 
-    def spread(x, t):
-        if not t:
-            return []
-        masks, size = _parts(common_mask(x, [e[0] for e in t]), len(t))
-        return [e + (masks[i], size) for i, e in enumerate(t)]
+    def engines(src, dsts):
+        return _count(common_mask(src, dsts))
 
     def halo_plan(x):
         t = []
-        if ok(x, right(x)):
-            t.append((right(x), 4 + W - 2, 0))
-        if ok(x, left(x)):
-            t.append((left(x), 4, 2))
-        return spread(x, t)
+        for nb, s, o in ((right(x), 4 + W - 2, 0), (left(x), 4, 2)):
+            if ok(x, nb):
+                t.append((nb, s, "HR", o, nb))
+            else:
+                t.append((hub_of[nb], s, "RL", o, nb))
+        t.sort(key=lambda e: 0 if e[2] == "RL" else 1)
+        return t
 
-    def pass_plan(h):
-        t = []
-        for c in clients:
-            if hub_of[c] == h and not ok(left(c), c):
-                t.append((c, left(c), 14, 0))
-            if hub_of[c] == h and not ok(right(c), c):
-                t.append((c, right(c), 8, 2))
-        return spread(h, t)
+    def relay_plan(h):
+        return [(x, e[3], e[4]) for x in range(N) for e in halo_plan(x) if e[2] == "RL" and e[0] == h]
 
     def dst(d):
         rid, pid = topo.addr(cores[d], core)
         return DstId(rid=rid, pnc=pid)
 
     is_hub = rank in hubs
-    F, Bz, A, E, C8, D, SQ, AB, Y, L = T.F, T.Bz, T.A, T.E, T.C8, T.D, T.SQ, T.AB, T.Y, T.L
-    vec = g.vector
-
-    g.sync.dma_start(F[:, 4:4 + W], T.u[:, :]).then_inc(sem.lu, 16)
-    g.scalar.dma_start(Bz[:, 4:4 + W], T.b[:, :]).then_inc(sem.lb, 16)
-
-    fills = [(F[:, 0:4], 0.0), (F[:, W + 4:W + 8], 0.0), (Bz[:, 0:4], 0.0), (Bz[:, W + 4:W + 8], 0.0),
-             (C8[:, :], 0.125), (T.PC2[:, :], 0.5), (T.PZ[:, :], 0.0)]
-    if is_hub:
-        fills += [(T.ZH[:, :, :], 0.0), (T.CS[:, 0:1], -1.0 / (N * W)), (T.CS[:, 1:2], 1.0)]
-    for ap, c in fills:
-        vec.memset(ap, c).then_inc(sem.ms, 1)
-    vec.wait_ge(sem.ms, len(fills))
-
+    F, Bz, A, U8, XS, D, Y, L = T.F, T.Bz, T.A, T.U8, T.XS, T.D, T.Y, T.L
+    PB, PT, PY = T.PB, T.PT, T.PY
+    vec, sc = g.vector, g.scalar
     st = {"v": 0, "w": 0, "sent": 0}
+
+    def send(to, src, out, rsem):
+        g.remote_dma_fused([RemoteDMATransfer(dst_ids=[dst(d) for d in to], dma_engine_mask=common_mask(rank, to),
+                                              remote_sem=rsem, srcs=[src], dsts=[out for d in to])], local_sem=sem.sent)
+        st["sent"] += engines(rank, to)
 
     def vwait():
         if st["w"] < st["v"]:
             vec.wait_ge(sem.v, st["v"])
             st["w"] = st["v"]
 
-    def tt(out, a, b, op, dep=True, sig=None):
-        if dep:
-            vwait()
-        ins = vec.tensor_tensor(out, a, b, op)
+    def done(ins, sig=None):
         if sig is None:
             ins.then_inc(sem.v, 1)
             st["v"] += 1
         else:
             ins.then_inc(sig, 1)
 
+    g.sync.dma_start(F[:, 4:4 + W], T.u[:, :]).then_inc(sem.lu, 16)
+    sc.dma_start(Bz[:, 4:4 + W], T.b[:, :]).then_inc(sem.lb, 16)
+
+    fills = [F[:, 0:4], F[:, W + 4:W + 8], Bz[:, 0:4], Bz[:, W + 4:W + 8], L[:, rank, 0:4]]
+    for ap in fills:
+        vec.memset(ap, 0.0).then_inc(sem.ms, 1)
+    vec.wait_ge(sem.ms, len(fills))
+    sc.wait_ge(sem.ms, len(fills))
+
+    sc.wait_ge(sem.lu, 16)
+    sc.activation(U8[:, :], F[:, 2:2 + X], ACT.Identity, scale=-8.0).then_inc(sem.sa, 1)
+    sc.wait_ge(sem.lb, 16)
+    sc.activation(PB[:, 0:X], Bz[:, 2:2 + X], ACT.Identity, scale=4.0).then_inc(sem.sa, 1)
+    sc.activation(T.HB[:, :], Bz[:, 4:4 + W], ACT.Identity, scale=0.5).then_inc(sem.hb, 1)
+
+    vec.wait_ge(sem.lu, 16)
+    done(vec.tensor_tensor(A[:, 0:X + 3], F[:, 0:X + 3], F[:, 1:X + 4], add))
+    vwait()
+    done(vec.tensor_tensor(PT[:, 0:X], A[:, 0:X], A[:, 3:X + 3], add))
+    vec.wait_ge(sem.sa, 2)
+    vwait()
+    done(vec.tensor_tensor(XS[:, :], PT[:, 0:X], U8[:, :], add))
+    vwait()
+    done(vec.tensor_tensor(D[:, :], PB[:, 4:W], XS[:, 4:W], add), sem.d)
+    done(vec.tensor_tensor(L[:, rank, 4:8], PB[:, 0:4], XS[:, 0:4], add), sem.msg)
+    done(vec.tensor_tensor(L[:, rank, 8:12], PB[:, W:W + 4], XS[:, W:W + 4], add), sem.msg)
+    vec.wait_ge(sem.d, 1)
+    done(vec.tensor_reduce(L[:, rank, 1:2], D[:, :], AX, mx, apply_absolute_value=True), sem.msg)
+    sc.wait_ge(sem.d, 1)
+    sc.activation(T.SQ[:, :], D[:, :], ACT.Square, scale=0.125, accum_out=L[:, rank, 0:1]).then_inc(sem.msg, 1)
+
     hp = halo_plan(rank)
     g.wait_ge(sem.lu, 16)
-    g.remote_dma_fused([RemoteDMATransfer(dst_ids=[dst(d)], dma_engine_mask=m, remote_sem=sem.hr,
-                                          srcs=[F[:, s:s + 2]], dsts=[T.HR[:, o:o + 2]])
-                        for d, s, o, m, _ in hp], local_sem=sem.sent)
-    st["sent"] += sum(p[4] for p in hp)
-
-    X = W + 4
-    vec.wait_ge(sem.lu, 16)
-    tt(A[:, 0:X + 3], F[:, 0:X + 3], F[:, 1:X + 4], add, dep=False)
-    vec.wait_ge(sem.lb, 16)
-    tt(T.PHB[:, :], Bz[:, 2:2 + X], T.PC2[:, :], mul, dep=False)
-    tt(T.PT[:, :], A[:, 0:X], A[:, 3:X + 3], add)
-    tt(E[:, :], T.PHB[:, :], F[:, 2:2 + X], sub, dep=False)
-    tt(T.PT8[:, :], T.PT[:, :], C8[:, :], mul)
-    tt(D[:, :], T.PT8[:, 4:W], E[:, 4:W], add)
-    tt(L[:, rank, 8:12], T.PT8[:, 0:4], E[:, 0:4], add, dep=False, sig=sem.msg)
-    tt(L[:, rank, 12:16], T.PT8[:, W:W + 4], E[:, W:W + 4], add, dep=False, sig=sem.msg)
-    tt(T.PND[:, :], T.PZ[:, :], D[:, :], sub)
-    tt(SQ[:, :], D[:, :], T.PND[:, :], mul)
-    tt(AB[:, :], D[:, :], T.PND[:, :], mx, dep=False)
-    n = W - 4
-    while n > 8:
-        h = n // 2
-        tt(SQ[:, 0:h], SQ[:, 0:h], SQ[:, n - h:n], add)
-        tt(AB[:, 0:h], AB[:, 0:h], AB[:, n - h:n], mx, dep=False)
-        n -= h
-    tt(L[:, rank, 0:4], SQ[:, 0:4], SQ[:, 4:8], add, sig=sem.msg)
-    tt(L[:, rank, 4:8], AB[:, 0:4], AB[:, 4:8], mx, dep=False, sig=sem.msg)
-
-    to = [h for h in hubs if h != rank]
-    m1, e1 = _parts(common_mask(rank, to), 1)
+    send([hp[0][0]], F[:, hp[0][1]:hp[0][1] + 2], T[hp[0][2]][:, hp[0][3]:hp[0][3] + 2], sem[hp[0][2].lower()])
     g.wait_ge(sem.msg, 4)
-    g.remote_dma_fused([RemoteDMATransfer(dst_ids=[dst(h) for h in to], dma_engine_mask=m1[0], remote_sem=sem.arr,
-                                          srcs=[L[:, rank, :]], dsts=[L[:, rank, :] for h in to])], local_sem=sem.sent)
-    st["sent"] += e1
+    send([h for h in hubs if h != rank], L[:, rank, :], L[:, rank, :], sem.arr)
+    send([hp[1][0]], F[:, hp[1][1]:hp[1][1] + 2], T[hp[1][2]][:, hp[1][3]:hp[1][3] + 2], sem[hp[1][2].lower()])
+    rp = relay_plan(rank)
+    if rp:
+        g.wait_ge(sem.rl, sum(engines(x, [rank]) for x, _, _ in rp))
+        for _, o, c in rp:
+            send([c], T.RL[:, o:o + 2], T.HR[:, o:o + 2], sem.hr)
 
-    tt(T.PY[:, :], T.PT8[:, 2:2 + W], E[:, 2:2 + W], add, dep=False)
-    tt(Y[:, :], T.PY[:, :], F[:, 4:4 + W], add)
-    raw_l, raw_r = ok(left(rank), rank), ok(right(rank), rank)
-    vec.wait_ge(sem.hr, sum(p[4] for x in (left(rank), right(rank)) for p in halo_plan(x) if p[0] == rank))
-    lo, hi = (0 if raw_l else 2), (4 if raw_r else 2)
-    G = T.G
-    tt(G[:, lo:hi], T.HR[:, lo:hi], C8[:, lo:hi], mul, dep=False)
-    if raw_l:
-        tt(Y[:, 0:2], Y[:, 0:2], G[:, 0:2], add)
-    if raw_r:
-        tt(Y[:, W - 2:W], Y[:, W - 2:W], G[:, 2:4], add, dep=not raw_l)
-    if raw_l:
-        tt(Y[:, 0:1], Y[:, 0:1], G[:, 1:2], add, sig=sem.yv)
-    if raw_r:
-        tt(Y[:, W - 1:W], Y[:, W - 1:W], G[:, 2:3], add, dep=not raw_l, sig=sem.yv)
+    done(vec.tensor_scalar(PY[:, 0:W], PT[:, 2:2 + W], 0.125, None, mul))
+    vec.wait_ge(sem.hb, 1)
+    vwait()
+    done(vec.tensor_tensor(Y[:, :], PY[:, 0:W], T.HB[:, :], add))
 
     if is_hub:
-        res = T.RES[:, 0:2]
-        arrived = sum(_parts(common_mask(x, [h for h in hubs if h != x]), 1)[1] for x in others(rank))
-        pp = pass_plan(rank)
-        if pp:
-            g.wait_ge(sem.arr, arrived)
-            g.remote_dma_fused([RemoteDMATransfer(dst_ids=[dst(d)], dma_engine_mask=m, remote_sem=sem.hq,
-                                                  srcs=[L[:, sl, s:s + 2]], dsts=[T.HQ[:, o:o + 2]])
-                                for d, sl, s, o, m, _ in pp], local_sem=sem.sent)
-            st["sent"] += sum(p[5] for p in pp)
+        arrived = sum(engines(x, [h for h in hubs if h != x]) for x in others(rank))
+        DB, SS, MM, RES = T.DB, T.SS, T.MM, T.RES
         vec.wait_ge(sem.arr, arrived)
         vec.wait_ge(sem.msg, 4)
-        DB, NDB, SQB, ABB, S1, M1, XX = T.DB, T.NDB, T.SQB, T.ABB, T.S1, T.M1, T.XX
-        tt(DB[:, 0:N - 1, :], L[:, 0:N - 1, 12:16], L[:, 1:N, 8:12], add)
-        tt(DB[:, N - 1, :], L[:, N - 1, 12:16], L[:, 0, 8:12], add, dep=False)
-        tt(NDB[:, :, :], T.ZH[:, :, :], DB[:, :, :], sub)
-        tt(SQB[:, :, :], DB[:, :, :], NDB[:, :, :], mul)
-        tt(ABB[:, :, :], DB[:, :, :], NDB[:, :, :], mx, dep=False)
-        tt(S1[:, :, :], L[:, :, 0:4], SQB[:, :, :], add)
-        tt(M1[:, :, :], L[:, :, 4:8], ABB[:, :, :], mx, dep=False)
-        n = N
-        while n > 2:
-            h = n // 2
-            tt(S1[:, 0:h, :], S1[:, 0:h, :], S1[:, n - h:n, :], add)
-            tt(M1[:, 0:h, :], M1[:, 0:h, :], M1[:, n - h:n, :], mx, dep=False)
-            n -= h
-        tt(S1[:, 0, :], S1[:, 0, :], S1[:, 1, :], add)
-        tt(M1[:, 0, :], M1[:, 0, :], M1[:, 1, :], mx, dep=False)
-        tt(S1[:, 0, 0:2], S1[:, 0, 0:2], S1[:, 0, 2:4], add)
-        tt(M1[:, 0, 0:2], M1[:, 0, 0:2], M1[:, 0, 2:4], mx, dep=False)
-        tt(XX[:, 0:1], S1[:, 0, 0:1], S1[:, 0, 1:2], add)
-        tt(XX[:, 1:2], M1[:, 0, 0:1], M1[:, 0, 1:2], mx, dep=False)
-        tt(res, XX[:, 0:2], T.CS[:, 0:2], mul, sig=sem.res)
-        mine = [c for c in clients if hub_of[c] == rank]
-        m2, e2 = _parts(common_mask(rank, mine), 1)
-        g.wait_ge(sem.res, 1)
-        g.remote_dma_fused([RemoteDMATransfer(dst_ids=[dst(c) for c in mine], dma_engine_mask=m2[0], remote_sem=sem.fin,
-                                              srcs=[res], dsts=[T.SD[:, :] for c in mine])], local_sem=sem.sent)
-        st["sent"] += e2
-        g.sync.wait_ge(sem.res, 1)
-        g.sync.dma_start(T.s[:, :], res).then_inc(sem.sts, 16)
+        done(vec.tensor_tensor(DB[:, 0:4 * (N - 1)], L[:, 0:N - 1, 8:12], L[:, 1:N, 4:8], add), sem.db)
+        done(vec.tensor_tensor(DB[:, 4 * (N - 1):4 * N], L[:, N - 1, 8:12], L[:, 0, 4:8], add), sem.db)
+        done(vec.tensor_reduce(MM[:, 0:1], L[:, :, 1], AX, mx))
+        vec.wait_ge(sem.db, 2)
+        done(vec.tensor_reduce(MM[:, 1:2], DB[:, :], AX, mx, apply_absolute_value=True))
+        sc.wait_ge(sem.arr, arrived)
+        sc.wait_ge(sem.msg, 4)
+        sc.activation(T.J1[:, :], L[:, :, 0], ACT.Identity, accum_out=SS[:, 0:1]).then_inc(sem.sf, 1)
+        sc.wait_ge(sem.db, 2)
+        sc.activation(T.J2[:, :], DB[:, :], ACT.Square, scale=0.125, accum_out=SS[:, 1:2]).then_inc(sem.sf, 1)
+        vwait()
+        done(vec.tensor_scalar(RES[:, 1:2], MM[:, 0:1], MM[:, 1:2], 0.125, mx, mul), sem.res)
+        vec.wait_ge(sem.sf, 2)
+        done(vec.tensor_scalar(RES[:, 0:1], SS[:, 0:1], SS[:, 1:2], 1.0 / (N * W), add, mul), sem.res)
+        g.wait_ge(sem.res, 2)
+        send([c for c in clients if hub_of[c] == rank], RES[:, 0:2], T.SD[:, :], sem.fin)
+        g.sync.wait_ge(sem.res, 2)
+        g.sync.dma_start(T.s[:, :], RES[:, 0:2]).then_inc(sem.sts, 16)
     else:
         hub = hub_of[rank]
-        fin = _parts(common_mask(hub, [c for c in clients if hub_of[c] == hub]), 1)[1]
-        for p in pass_plan(hub):
-            if p[0] == rank:
-                a = 0 if p[3] == 0 else W - 2
-                vec.wait_ge(sem.hq, p[5])
-                tt(Y[:, a:a + 2], Y[:, a:a + 2], T.HQ[:, p[3]:p[3] + 2], add, sig=sem.yv)
-        g.sync.wait_ge(sem.fin, fin)
+        g.sync.wait_ge(sem.fin, engines(hub, [c for c in clients if hub_of[c] == hub]))
         g.sync.dma_start(T.s[:, :], T.SD[:, :]).then_inc(sem.sts, 16)
-    g.scalar.wait_ge(sem.yv, 2)
-    g.scalar.dma_start(T.y[:, :], Y[:, :]).then_inc(sem.sty, 16)
 
+    G = T.G
+    vec.wait_ge(sem.hr, sum(engines(x if e[2] == "HR" else e[0], [rank])
+                            for x in (left(rank), right(rank)) for e in halo_plan(x) if e[4] == rank))
+    done(vec.tensor_scalar(G[:, :], T.HR[:, :], 0.125, None, mul))
     vwait()
+    done(vec.tensor_tensor(Y[:, 0:2], Y[:, 0:2], G[:, 0:2], add))
+    done(vec.tensor_tensor(Y[:, W - 2:W], Y[:, W - 2:W], G[:, 2:4], add))
+    vwait()
+    done(vec.tensor_tensor(Y[:, 0:1], Y[:, 0:1], G[:, 1:2], add), sem.yv)
+    done(vec.tensor_tensor(Y[:, W - 1:W], Y[:, W - 1:W], G[:, 2:3], add), sem.yv)
+    sc.wait_ge(sem.yv, 2)
+    sc.dma_start(T.y[:, :], Y[:, :]).then_inc(sem.sty, 16)
+
     g.wait_ge(sem.sent, st["sent"])
     g.sync.wait_ge(sem.sts, 16)
-    g.scalar.wait_ge(sem.sty, 16)
+    sc.wait_ge(sem.sty, 16)

@@ -3,34 +3,33 @@ from concourse.mybir import AluOpType, AxisListType, ActivationFunctionType
 
 N, W = 9, 64
 K = 12
+M = 10
 X = W + 4
+U0 = 8
 SCRATCH = {
-    "F": ("sbuf", [128, W + 8], "float32"),
+    "F": ("sbuf", [128, W + 12], "float32"),
     "Bz": ("sbuf", [128, W + 8], "float32"),
-    "A": ("sbuf", [128, W + 8], "float32"),
-    "U8": ("sbuf", [128, X], "float32"),
+    "U9": ("sbuf", [128, X], "float32"),
     "XS": ("sbuf", [128, X], "float32"),
-    "D": ("sbuf", [128, W - 4], "float32"),
+    "D": ("sbuf", [128, X], "float32"),
     "SQ": ("sbuf", [128, W - 4], "float32"),
-    "HB": ("sbuf", [128, W], "float32"),
     "Y": ("sbuf", [128, W], "float32"),
-    "L": ("sbuf", [128, N, K], "float32"),
+    "L": ("sbuf", [128, N + 1, K], "float32"),
     "HR": ("sbuf", [128, 4], "float32"),
     "G": ("sbuf", [128, 4], "float32"),
     "RL": ("sbuf", [128, 4], "float32"),
     "SD": ("dram", [128, 2], "float32"),
-    "DB": ("sbuf", [128, 4 * N], "float32"),
+    "Z": ("sbuf", [128, 5 * N], "float32"),
     "J1": ("sbuf", [128, N], "float32"),
     "J2": ("sbuf", [128, 4 * N], "float32"),
     "SS": ("sbuf", [128, 4], "float32"),
-    "MM": ("sbuf", [128, 4], "float32"),
     "RES": ("sbuf", [128, 4], "float32"),
     "PB": ("psum", [128, 512], "float32"),
     "PT": ("psum", [128, 512], "float32"),
     "PY": ("psum", [128, 512], "float32"),
 }
-SEMAPHORES = ["lu", "lb", "ms", "v", "sa", "hb", "d", "msg", "arr", "hr", "rl", "db", "sf", "fin", "res", "yv", "sent",
-              "sts", "sty"]
+SEMAPHORES = ["lu", "lb", "ms", "v", "sa", "sb", "d", "msg", "dup", "yd", "arr", "hr", "rl", "db", "zc", "sf", "fin", "res",
+              "yv", "sent", "sts", "sty"]
 
 
 def _count(m):
@@ -43,7 +42,7 @@ def rank_program(g, core, T, topo):
         return
     cores = list(T.cores)
     sem = T.sem
-    add, mul, mx = AluOpType.add, AluOpType.mult, AluOpType.max
+    add, sub, mul, mx = AluOpType.add, AluOpType.subtract, AluOpType.mult, AluOpType.max
     AX = AxisListType.X
     ACT = ActivationFunctionType
     others = lambda r: [x for x in range(N) if x != r]
@@ -51,12 +50,27 @@ def rank_program(g, core, T, topo):
 
     hubs = [r for r in range(N) if all(ok(r, x) and ok(x, r) for x in others(r))]
     clients = [r for r in range(N) if r not in hubs]
-    load = dict((h, 0) for h in hubs)
+    room = dict((h, 0) for h in hubs)
+    left_over = len(clients)
+    while left_over:
+        for i, h in enumerate(hubs):
+            take = min(left_over, max(0, len(hubs) - i - room[h])) if room[h] < len(hubs) - i else 0
+            room[h] += take
+            left_over -= take
+        if left_over:
+            for h in hubs:
+                if left_over:
+                    room[h] += 1
+                    left_over -= 1
+    rack_of = lambda r: topo.rack(topo.host(cores[r]))
+    same_chip_no = lambda a, b: topo.chip(cores[a]) == topo.chip(cores[b])
     hub_of = {}
-    for c in clients:
-        h = min(hubs, key=lambda h: (load[h], 0 if topo.chip(cores[h]) == topo.chip(cores[c]) else 1, h))
+    for c in sorted(clients, key=lambda c: (0 if rack_of(c) != rack_of(hubs[0]) else 1, c)):
+        h = min([h for h in hubs if room[h] > 0], key=lambda h: (0 if same_chip_no(h, c) else 1, -room[h], h))
         hub_of[c] = h
-        load[h] += 1
+        room[h] -= 1
+    served = lambda h: [c for c in clients if hub_of[c] == h]
+    relay = min(hubs, key=lambda h: (len(served(h)), -hubs.index(h)))
     left = lambda r: (r - 1) % N
     right = lambda r: (r + 1) % N
 
@@ -71,11 +85,11 @@ def rank_program(g, core, T, topo):
 
     def halo_plan(x):
         t = []
-        for nb, s, o in ((right(x), 4 + W - 2, 0), (left(x), 4, 2)):
+        for nb, s, o in ((right(x), U0 + W - 2, 0), (left(x), U0, 2)):
             if ok(x, nb):
                 t.append((nb, s, "HR", o, nb))
             else:
-                t.append((hub_of[nb], s, "RL", o, nb))
+                t.append((relay, s, "RL", o, nb))
         t.sort(key=lambda e: 0 if e[2] == "RL" else 1)
         return t
 
@@ -87,14 +101,14 @@ def rank_program(g, core, T, topo):
         return DstId(rid=rid, pnc=pid)
 
     is_hub = rank in hubs
-    F, Bz, A, U8, XS, D, Y, L = T.F, T.Bz, T.A, T.U8, T.XS, T.D, T.Y, T.L
+    F, Bz, U9, XS, D, Y, L = T.F, T.Bz, T.U9, T.XS, T.D, T.Y, T.L
     PB, PT, PY = T.PB, T.PT, T.PY
     vec, sc = g.vector, g.scalar
     st = {"v": 0, "w": 0, "sent": 0}
 
-    def send(to, src, out, rsem):
+    def send(to, src, outs, rsem):
         g.remote_dma_fused([RemoteDMATransfer(dst_ids=[dst(d) for d in to], dma_engine_mask=common_mask(rank, to),
-                                              remote_sem=rsem, srcs=[src], dsts=[out for d in to])], local_sem=sem.sent)
+                                              remote_sem=rsem, srcs=[src], dsts=outs)], local_sem=sem.sent)
         st["sent"] += engines(rank, to)
 
     def vwait():
@@ -109,80 +123,81 @@ def rank_program(g, core, T, topo):
         else:
             ins.then_inc(sig, 1)
 
-    g.sync.dma_start(F[:, 4:4 + W], T.u[:, :]).then_inc(sem.lu, 16)
+    g.sync.dma_start(F[:, U0:U0 + W], T.u[:, :]).then_inc(sem.lu, 16)
     sc.dma_start(Bz[:, 4:4 + W], T.b[:, :]).then_inc(sem.lb, 16)
 
-    fills = [F[:, 0:4], F[:, W + 4:W + 8], Bz[:, 0:4], Bz[:, W + 4:W + 8], L[:, rank, 0:4]]
+    fills = [F[:, 0:U0], F[:, U0 + W:U0 + W + 4], Bz[:, 0:4], Bz[:, W + 4:W + 8]]
     for ap in fills:
         vec.memset(ap, 0.0).then_inc(sem.ms, 1)
     vec.wait_ge(sem.ms, len(fills))
     sc.wait_ge(sem.ms, len(fills))
 
     sc.wait_ge(sem.lu, 16)
-    sc.activation(U8[:, :], F[:, 2:2 + X], ACT.Identity, scale=-8.0).then_inc(sem.sa, 1)
+    sc.activation(U9[:, :], F[:, U0 - 2:U0 - 2 + X], ACT.Identity, scale=-9.0).then_inc(sem.sa, 1)
     sc.wait_ge(sem.lb, 16)
-    sc.activation(PB[:, 0:X], Bz[:, 2:2 + X], ACT.Identity, scale=4.0).then_inc(sem.sa, 1)
-    sc.activation(T.HB[:, :], Bz[:, 4:4 + W], ACT.Identity, scale=0.5).then_inc(sem.hb, 1)
+    sc.activation(PB[:, 0:X], Bz[:, 2:2 + X], ACT.Identity, scale=4.0).then_inc(sem.sb, 1)
 
     vec.wait_ge(sem.lu, 16)
-    done(vec.tensor_tensor(A[:, 0:X + 3], F[:, 0:X + 3], F[:, 1:X + 4], add))
+    done(vec.tensor_tensor_scan(PT[:, 0:X], F[:, U0:U0 + X], F[:, U0 - 5:U0 - 5 + X], 0.0, add, sub))
+    vec.wait_ge(sem.sa, 1)
     vwait()
-    done(vec.tensor_tensor(PT[:, 0:X], A[:, 0:X], A[:, 3:X + 3], add))
-    vec.wait_ge(sem.sa, 2)
+    done(vec.tensor_tensor(XS[:, :], PT[:, 0:X], U9[:, :], add))
+    vec.wait_ge(sem.sb, 1)
     vwait()
-    done(vec.tensor_tensor(XS[:, :], PT[:, 0:X], U8[:, :], add))
-    vwait()
-    done(vec.tensor_tensor(D[:, :], PB[:, 4:W], XS[:, 4:W], add), sem.d)
-    done(vec.tensor_tensor(L[:, rank, 4:8], PB[:, 0:4], XS[:, 0:4], add), sem.msg)
-    done(vec.tensor_tensor(L[:, rank, 8:12], PB[:, W:W + 4], XS[:, W:W + 4], add), sem.msg)
+    done(vec.tensor_tensor(D[:, :], PB[:, 0:X], XS[:, :], add), sem.d)
     vec.wait_ge(sem.d, 1)
-    done(vec.tensor_reduce(L[:, rank, 1:2], D[:, :], AX, mx, apply_absolute_value=True), sem.msg)
+    done(vec.tensor_reduce(L[:, 0, 9:10], D[:, 4:W], AX, mx, apply_absolute_value=True), sem.msg)
+    done(vec.tensor_scalar(L[:, 0, 4:8], D[:, W:W + 4], 0.125, None, mul), sem.msg)
     sc.wait_ge(sem.d, 1)
-    sc.activation(T.SQ[:, :], D[:, :], ACT.Square, scale=0.125, accum_out=L[:, rank, 0:1]).then_inc(sem.msg, 1)
+    sc.activation(T.SQ[:, :], D[:, 4:W], ACT.Square, scale=0.125, accum_out=L[:, 0, 8:9]).then_inc(sem.msg, 1)
+    sc.activation(L[:, 0, 0:4], D[:, 0:4], ACT.Identity, scale=0.125).then_inc(sem.msg, 1)
+    if is_hub:
+        sc.activation(L[:, N, 0:4], D[:, 0:4], ACT.Identity, scale=0.125).then_inc(sem.dup, 1)
+    sc.activation(PY[:, 0:W], D[:, 2:2 + W], ACT.Identity, scale=0.125).then_inc(sem.yd, 1)
 
     hp = halo_plan(rank)
     g.wait_ge(sem.lu, 16)
-    send([hp[0][0]], F[:, hp[0][1]:hp[0][1] + 2], T[hp[0][2]][:, hp[0][3]:hp[0][3] + 2], sem[hp[0][2].lower()])
+    send([hp[0][0]], F[:, hp[0][1]:hp[0][1] + 2], [T[hp[0][2]][:, hp[0][3]:hp[0][3] + 2]], sem[hp[0][2].lower()])
     g.wait_ge(sem.msg, 4)
-    send([h for h in hubs if h != rank], L[:, rank, :], L[:, rank, :], sem.arr)
-    send([hp[1][0]], F[:, hp[1][1]:hp[1][1] + 2], T[hp[1][2]][:, hp[1][3]:hp[1][3] + 2], sem[hp[1][2].lower()])
+    to = [h for h in hubs if h != rank]
+    send(to, L[:, 0, 0:M], [L[:, (rank - h) % N, 0:M] for h in to], sem.arr)
+    send([hp[1][0]], F[:, hp[1][1]:hp[1][1] + 2], [T[hp[1][2]][:, hp[1][3]:hp[1][3] + 2]], sem[hp[1][2].lower()])
     rp = relay_plan(rank)
     if rp:
         g.wait_ge(sem.rl, sum(engines(x, [rank]) for x, _, _ in rp))
         for _, o, c in rp:
-            send([c], T.RL[:, o:o + 2], T.HR[:, o:o + 2], sem.hr)
+            send([c], T.RL[:, o:o + 2], [T.HR[:, o:o + 2]], sem.hr)
 
-    done(vec.tensor_scalar(PY[:, 0:W], PT[:, 2:2 + W], 0.125, None, mul))
-    vec.wait_ge(sem.hb, 1)
-    vwait()
-    done(vec.tensor_tensor(Y[:, :], PY[:, 0:W], T.HB[:, :], add))
+    vec.wait_ge(sem.yd, 1)
+    done(vec.tensor_tensor(Y[:, :], PY[:, 0:W], F[:, U0:U0 + W], add))
 
     if is_hub:
         arrived = sum(engines(x, [h for h in hubs if h != x]) for x in others(rank))
-        DB, SS, MM, RES = T.DB, T.SS, T.MM, T.RES
+        Z, SS, RES = T.Z, T.SS, T.RES
+        E = 4 * N
         vec.wait_ge(sem.arr, arrived)
         vec.wait_ge(sem.msg, 4)
-        done(vec.tensor_tensor(DB[:, 0:4 * (N - 1)], L[:, 0:N - 1, 8:12], L[:, 1:N, 4:8], add), sem.db)
-        done(vec.tensor_tensor(DB[:, 4 * (N - 1):4 * N], L[:, N - 1, 8:12], L[:, 0, 4:8], add), sem.db)
-        done(vec.tensor_reduce(MM[:, 0:1], L[:, :, 1], AX, mx))
-        vec.wait_ge(sem.db, 2)
-        done(vec.tensor_reduce(MM[:, 1:2], DB[:, :], AX, mx, apply_absolute_value=True))
+        vec.wait_ge(sem.dup, 1)
+        done(vec.tensor_tensor(Z[:, 0:E], L[:, 0:N, 4:8], L[:, 1:N + 1, 0:4], add), sem.db)
         sc.wait_ge(sem.arr, arrived)
         sc.wait_ge(sem.msg, 4)
-        sc.activation(T.J1[:, :], L[:, :, 0], ACT.Identity, accum_out=SS[:, 0:1]).then_inc(sem.sf, 1)
-        sc.wait_ge(sem.db, 2)
-        sc.activation(T.J2[:, :], DB[:, :], ACT.Square, scale=0.125, accum_out=SS[:, 1:2]).then_inc(sem.sf, 1)
-        vwait()
-        done(vec.tensor_scalar(RES[:, 1:2], MM[:, 0:1], MM[:, 1:2], 0.125, mx, mul), sem.res)
-        vec.wait_ge(sem.sf, 2)
-        done(vec.tensor_scalar(RES[:, 0:1], SS[:, 0:1], SS[:, 1:2], 1.0 / (N * W), add, mul), sem.res)
+        sc.activation(Z[:, E:E + N], L[:, 0:N, 9], ACT.Identity, scale=0.125).then_inc(sem.zc, 1)
+        vec.wait_ge(sem.db, 1)
+        vec.wait_ge(sem.zc, 1)
+        done(vec.tensor_reduce(RES[:, 1:2], Z[:, 0:E + N], AX, mx, apply_absolute_value=True), sem.res)
+        sc.wait_ge(sem.db, 1)
+        sc.activation(T.J2[:, :], Z[:, 0:E], ACT.Square, scale=1.0 / 72.0, accum_out=SS[:, 0:1]).then_inc(sem.sf, 1)
+        sc.wait_ge(sem.sf, 1)
+        sc.activation(T.J1[:, :], L[:, 0:N, 8], ACT.Identity, bias=SS[:, 0:1], scale=1.0 / (N * W),
+                      accum_out=RES[:, 0:1]).then_inc(sem.res, 1)
         g.wait_ge(sem.res, 2)
-        send([c for c in clients if hub_of[c] == rank], RES[:, 0:2], T.SD[:, :], sem.fin)
+        mine = served(rank)
+        send(mine, RES[:, 0:2], [T.SD[:, :] for c in mine], sem.fin)
         g.sync.wait_ge(sem.res, 2)
         g.sync.dma_start(T.s[:, :], RES[:, 0:2]).then_inc(sem.sts, 16)
     else:
         hub = hub_of[rank]
-        g.sync.wait_ge(sem.fin, engines(hub, [c for c in clients if hub_of[c] == hub]))
+        g.sync.wait_ge(sem.fin, engines(hub, served(hub)))
         g.sync.dma_start(T.s[:, :], T.SD[:, :]).then_inc(sem.sts, 16)
 
     G = T.G

from concourse.bass import DstId, RemoteDMATransfer
from concourse.mybir import AluOpType, AxisListType, ActivationFunctionType

N, W = 9, 64
K = 12
M = 10
X = W + 4
U0 = 8
SCRATCH = {
    "F": ("sbuf", [128, W + 12], "float32"),
    "Bz": ("sbuf", [128, W + 8], "float32"),
    "U9": ("sbuf", [128, X], "float32"),
    "XS": ("sbuf", [128, X], "float32"),
    "D": ("sbuf", [128, X], "float32"),
    "SQ": ("sbuf", [128, W - 4], "float32"),
    "Y": ("sbuf", [128, W], "float32"),
    "L": ("sbuf", [128, N + 1, K], "float32"),
    "HR": ("sbuf", [128, 4], "float32"),
    "G": ("sbuf", [128, 4], "float32"),
    "RL": ("sbuf", [128, 4], "float32"),
    "SD": ("dram", [128, 2], "float32"),
    "Z": ("sbuf", [128, 5 * N], "float32"),
    "J1": ("sbuf", [128, N], "float32"),
    "J2": ("sbuf", [128, 4 * N], "float32"),
    "SS": ("sbuf", [128, 4], "float32"),
    "RES": ("sbuf", [128, 4], "float32"),
    "PB": ("psum", [128, 512], "float32"),
    "PT": ("psum", [128, 512], "float32"),
    "PY": ("psum", [128, 512], "float32"),
}
SEMAPHORES = ["lu", "lb", "ms", "v", "sa", "sb", "d", "msg", "dup", "yd", "arr", "hr", "rl", "db", "zc", "sf", "fin", "res",
              "yv", "sent", "sts", "sty"]


def _count(m):
    return sum((m >> i) & 1 for i in range(16))


def rank_program(g, core, T, topo):
    rank = T.rank_of(core)
    if rank is None:
        return
    cores = list(T.cores)
    sem = T.sem
    add, sub, mul, mx = AluOpType.add, AluOpType.subtract, AluOpType.mult, AluOpType.max
    AX = AxisListType.X
    ACT = ActivationFunctionType
    others = lambda r: [x for x in range(N) if x != r]
    ok = lambda a, b: topo.may_write(cores[a], cores[b])

    hubs = [r for r in range(N) if all(ok(r, x) and ok(x, r) for x in others(r))]
    clients = [r for r in range(N) if r not in hubs]
    room = dict((h, 0) for h in hubs)
    left_over = len(clients)
    while left_over:
        for i, h in enumerate(hubs):
            take = min(left_over, max(0, len(hubs) - i - room[h])) if room[h] < len(hubs) - i else 0
            room[h] += take
            left_over -= take
        if left_over:
            for h in hubs:
                if left_over:
                    room[h] += 1
                    left_over -= 1
    rack_of = lambda r: topo.rack(topo.host(cores[r]))
    same_chip_no = lambda a, b: topo.chip(cores[a]) == topo.chip(cores[b])
    hub_of = {}
    for c in sorted(clients, key=lambda c: (0 if rack_of(c) != rack_of(hubs[0]) else 1, c)):
        h = min([h for h in hubs if room[h] > 0], key=lambda h: (0 if same_chip_no(h, c) else 1, -room[h], h))
        hub_of[c] = h
        room[h] -= 1
    served = lambda h: [c for c in clients if hub_of[c] == h]
    relay = min(hubs, key=lambda h: (len(served(h)), -hubs.index(h)))
    left = lambda r: (r - 1) % N
    right = lambda r: (r + 1) % N

    def common_mask(src, dsts):
        m = topo.mask(cores[src], cores[dsts[0]])
        for d in dsts[1:]:
            m &= topo.mask(cores[src], cores[d])
        return m

    def engines(src, dsts):
        return _count(common_mask(src, dsts))

    def halo_plan(x):
        t = []
        for nb, s, o in ((right(x), U0 + W - 2, 0), (left(x), U0, 2)):
            if ok(x, nb):
                t.append((nb, s, "HR", o, nb))
            else:
                t.append((relay, s, "RL", o, nb))
        t.sort(key=lambda e: 0 if e[2] == "RL" else 1)
        return t

    def relay_plan(h):
        return [(x, e[3], e[4]) for x in range(N) for e in halo_plan(x) if e[2] == "RL" and e[0] == h]

    def dst(d):
        rid, pid = topo.addr(cores[d], core)
        return DstId(rid=rid, pnc=pid)

    is_hub = rank in hubs
    F, Bz, U9, XS, D, Y, L = T.F, T.Bz, T.U9, T.XS, T.D, T.Y, T.L
    PB, PT, PY = T.PB, T.PT, T.PY
    vec, sc = g.vector, g.scalar
    st = {"v": 0, "w": 0, "sent": 0}

    def send(to, src, outs, rsem):
        g.remote_dma_fused([RemoteDMATransfer(dst_ids=[dst(d) for d in to], dma_engine_mask=common_mask(rank, to),
                                              remote_sem=rsem, srcs=[src], dsts=outs)], local_sem=sem.sent)
        st["sent"] += engines(rank, to)

    def vwait():
        if st["w"] < st["v"]:
            vec.wait_ge(sem.v, st["v"])
            st["w"] = st["v"]

    def done(ins, sig=None):
        if sig is None:
            ins.then_inc(sem.v, 1)
            st["v"] += 1
        else:
            ins.then_inc(sig, 1)

    g.sync.dma_start(F[:, U0:U0 + W], T.u[:, :]).then_inc(sem.lu, 16)
    sc.dma_start(Bz[:, 4:4 + W], T.b[:, :]).then_inc(sem.lb, 16)

    fills = [F[:, 0:U0], F[:, U0 + W:U0 + W + 4], Bz[:, 0:4], Bz[:, W + 4:W + 8]]
    for ap in fills:
        vec.memset(ap, 0.0).then_inc(sem.ms, 1)
    vec.wait_ge(sem.ms, len(fills))
    sc.wait_ge(sem.ms, len(fills))

    sc.wait_ge(sem.lu, 16)
    sc.activation(U9[:, :], F[:, U0 - 2:U0 - 2 + X], ACT.Identity, scale=-9.0).then_inc(sem.sa, 1)
    sc.wait_ge(sem.lb, 16)
    sc.activation(PB[:, 0:X], Bz[:, 2:2 + X], ACT.Identity, scale=4.0).then_inc(sem.sb, 1)

    vec.wait_ge(sem.lu, 16)
    done(vec.tensor_tensor_scan(PT[:, 0:X], F[:, U0:U0 + X], F[:, U0 - 5:U0 - 5 + X], 0.0, add, sub))
    vec.wait_ge(sem.sa, 1)
    vwait()
    done(vec.tensor_tensor(XS[:, :], PT[:, 0:X], U9[:, :], add))
    vec.wait_ge(sem.sb, 1)
    vwait()
    done(vec.tensor_tensor(D[:, :], PB[:, 0:X], XS[:, :], add), sem.d)
    vec.wait_ge(sem.d, 1)
    done(vec.tensor_reduce(L[:, 0, 9:10], D[:, 4:W], AX, mx, apply_absolute_value=True), sem.msg)
    done(vec.tensor_scalar(L[:, 0, 4:8], D[:, W:W + 4], 0.125, None, mul), sem.msg)
    sc.wait_ge(sem.d, 1)
    sc.activation(T.SQ[:, :], D[:, 4:W], ACT.Square, scale=0.125, accum_out=L[:, 0, 8:9]).then_inc(sem.msg, 1)
    sc.activation(L[:, 0, 0:4], D[:, 0:4], ACT.Identity, scale=0.125).then_inc(sem.msg, 1)
    if is_hub:
        sc.activation(L[:, N, 0:4], D[:, 0:4], ACT.Identity, scale=0.125).then_inc(sem.dup, 1)
    sc.activation(PY[:, 0:W], D[:, 2:2 + W], ACT.Identity, scale=0.125).then_inc(sem.yd, 1)

    hp = halo_plan(rank)
    g.wait_ge(sem.lu, 16)
    send([hp[0][0]], F[:, hp[0][1]:hp[0][1] + 2], [T[hp[0][2]][:, hp[0][3]:hp[0][3] + 2]], sem[hp[0][2].lower()])
    g.wait_ge(sem.msg, 4)
    to = [h for h in hubs if h != rank]
    send(to, L[:, 0, 0:M], [L[:, (rank - h) % N, 0:M] for h in to], sem.arr)
    send([hp[1][0]], F[:, hp[1][1]:hp[1][1] + 2], [T[hp[1][2]][:, hp[1][3]:hp[1][3] + 2]], sem[hp[1][2].lower()])
    rp = relay_plan(rank)
    if rp:
        g.wait_ge(sem.rl, sum(engines(x, [rank]) for x, _, _ in rp))
        for _, o, c in rp:
            send([c], T.RL[:, o:o + 2], [T.HR[:, o:o + 2]], sem.hr)

    vec.wait_ge(sem.yd, 1)
    done(vec.tensor_tensor(Y[:, :], PY[:, 0:W], F[:, U0:U0 + W], add))

    if is_hub:
        arrived = sum(engines(x, [h for h in hubs if h != x]) for x in others(rank))
        Z, SS, RES = T.Z, T.SS, T.RES
        E = 4 * N
        vec.wait_ge(sem.arr, arrived)
        vec.wait_ge(sem.msg, 4)
        vec.wait_ge(sem.dup, 1)
        done(vec.tensor_tensor(Z[:, 0:E], L[:, 0:N, 4:8], L[:, 1:N + 1, 0:4], add), sem.db)
        sc.wait_ge(sem.arr, arrived)
        sc.wait_ge(sem.msg, 4)
        sc.activation(Z[:, E:E + N], L[:, 0:N, 9], ACT.Identity, scale=0.125).then_inc(sem.zc, 1)
        vec.wait_ge(sem.db, 1)
        vec.wait_ge(sem.zc, 1)
        done(vec.tensor_reduce(RES[:, 1:2], Z[:, 0:E + N], AX, mx, apply_absolute_value=True), sem.res)
        sc.wait_ge(sem.db, 1)
        sc.activation(T.J2[:, :], Z[:, 0:E], ACT.Square, scale=1.0 / 72.0, accum_out=SS[:, 0:1]).then_inc(sem.sf, 1)
        sc.wait_ge(sem.sf, 1)
        sc.activation(T.J1[:, :], L[:, 0:N, 8], ACT.Identity, bias=SS[:, 0:1], scale=1.0 / (N * W),
                      accum_out=RES[:, 0:1]).then_inc(sem.res, 1)
        g.wait_ge(sem.res, 2)
        mine = served(rank)
        send(mine, RES[:, 0:2], [T.SD[:, :] for c in mine], sem.fin)
        g.sync.wait_ge(sem.res, 2)
        g.sync.dma_start(T.s[:, :], RES[:, 0:2]).then_inc(sem.sts, 16)
    else:
        hub = hub_of[rank]
        g.sync.wait_ge(sem.fin, engines(hub, served(hub)))
        g.sync.dma_start(T.s[:, :], T.SD[:, :]).then_inc(sem.sts, 16)

    G = T.G
    vec.wait_ge(sem.hr, sum(engines(x if e[2] == "HR" else e[0], [rank])
                            for x in (left(rank), right(rank)) for e in halo_plan(x) if e[4] == rank))
    done(vec.tensor_scalar(G[:, :], T.HR[:, :], 0.125, None, mul))
    vwait()
    done(vec.tensor_tensor(Y[:, 0:2], Y[:, 0:2], G[:, 0:2], add))
    done(vec.tensor_tensor(Y[:, W - 2:W], Y[:, W - 2:W], G[:, 2:4], add))
    vwait()
    done(vec.tensor_tensor(Y[:, 0:1], Y[:, 0:1], G[:, 1:2], add), sem.yv)
    done(vec.tensor_tensor(Y[:, W - 1:W], Y[:, W - 1:W], G[:, 2:3], add), sem.yv)
    sc.wait_ge(sem.yv, 2)
    sc.dma_start(T.y[:, :], Y[:, :]).then_inc(sem.sty, 16)

    g.wait_ge(sem.sent, st["sent"])
    g.sync.wait_ge(sem.sts, 16)
    sc.wait_ge(sem.sty, 16)
